import numpy as np
import ml_dtypes


def mxq(x, axis, fmt="e4m3"):
    dtype, down = {"e4m3": (ml_dtypes.float8_e4m3fn, 7), "e5m2": (ml_dtypes.float8_e5m2, 14)}[fmt]
    v = np.moveaxis(np.asarray(x, np.float32).astype(ml_dtypes.bfloat16).astype(np.float64), axis, -1)
    blocks = v.reshape(v.shape[:-1] + (-1, 32))
    amax = np.abs(blocks).max(-1, keepdims=True)
    byte = np.maximum(np.where(amax > 0, np.frexp(amax)[1] - 1 + 127, 0) - down, 1)
    scale = np.exp2(byte - 127.0)
    codes = (blocks / scale).astype(np.float32).astype(dtype).astype(np.float64)
    return np.moveaxis((codes * scale).reshape(v.shape), -1, axis)


WIDE = False


def mx_kscale(k):
    if not WIDE:
        return np.ones(k)
    levels = np.array([10, -10, 5, -5, 0])
    if k % 512:
        return np.exp2(np.random.permutation(np.resize(levels, k // 32))).repeat(32)
    a = np.empty((k // 512, 16))
    for p in range(k // 512):
        a[p, :8] = np.random.permutation(np.resize(levels, 8))
        for g in range(8):
            far = levels[np.abs(levels - a[p, g]) >= 10]
            a[p, g + 8] = far[np.random.randint(len(far))]
    return np.exp2(a.ravel()).repeat(32)


BF16 = ml_dtypes.bfloat16


def bf(x):
    return np.asarray(x, np.float32).astype(BF16)


def f64(x):
    return np.asarray(x).astype(np.float64)


E2M1 = np.array([0.0, 0.5, 1.0, 1.5, 2.0, 3.0, 4.0, 6.0, -0.0, -0.5, -1.0, -1.5, -2.0, -3.0, -4.0, -6.0])


def pack_weight(w, fmt):
    k, n = w.shape
    w = f64(bf(w)).reshape(k // 32, 32, n)
    amax = np.abs(w).max(1)
    if fmt == "e4m3":
        byte = np.frexp(amax)[1] - 1 + 127 - 7
    else:
        mant, ex = np.frexp(amax / 6.0)
        byte = np.where(mant > 0.5, ex, ex - 1) + 127
    byte = np.clip(np.where(amax > 0, byte, 1), 1, 254)
    scaled = (w * np.exp2(127.0 - byte)[:, None, :]).reshape(k, n).astype(np.float32)
    by_word = np.ascontiguousarray(scaled.reshape(k // 512, 128, 4, n).transpose(0, 1, 3, 2))
    if fmt == "e4m3":
        words = by_word.astype(ml_dtypes.float8_e4m3fn).view(np.uint8)
    else:
        c = by_word.astype(ml_dtypes.float4_e2m1fn).view(np.uint8) & 0xF
        words = c[..., 0::2] | (c[..., 1::2] << 4)
    return np.ascontiguousarray(words), np.ascontiguousarray(byte.astype(np.uint8).reshape(k // 512, 16, n))


def unpack_weight(words, scales, fmt):
    g, p, n, _ = words.shape
    if fmt == "e4m3":
        vals = np.ascontiguousarray(words).view(ml_dtypes.float8_e4m3fn).astype(np.float64)
    else:
        nib = np.empty((g, p, n, 4), np.uint8)
        nib[..., 0::2] = words & 0xF
        nib[..., 1::2] = words >> 4
        vals = E2M1[nib]
    vals = vals * np.repeat(np.exp2(scales.astype(np.float64) - 127.0), 8, axis=1)[..., None]
    return vals.transpose(0, 1, 3, 2).reshape(g * 512, n)
def pack4(w):
    words, scales = pack_weight(w, "e2m1")
    return words.reshape(words.shape[0], 128, -1), scales


def unpack4(words, scales):
    return unpack_weight(words.reshape(words.shape[0], 128, -1, 2), scales, "e2m1")


E4M3FN = np.array([(-1.0 if i & 128 else 1.0) * ((1.0 + (i & 7) / 8.0) * 2.0 ** (((i >> 3) & 15) - 7) if i & 120 else (i & 7) * 2.0 ** -9) for i in range(256)])


def e4m3fn_bytes(y):
    return np.clip(np.asarray(y, np.float64), -448.0, 448.0).astype(np.float32).astype(ml_dtypes.float8_e4m3fn).view(np.uint8)


def e4m3fn_values(b):
    return E4M3FN[b]


N, D, H, Z, C = 512, 1024, 512, 128, 128
CZ = C * Z


def index_hidden(phiq, z, wp, wz, b):
    zw = np.sum(z[:, :, None] * wz[None, :, :], axis=1)
    return np.maximum((phiq @ wp) + zw + b, 0.0)


def draw0():
    s, t = mx_kscale(D), mx_kscale(H)
    phi = bf(np.random.standard_normal((N, D)) * s)
    z = bf(np.random.standard_normal((N, Z)))
    wp_words, wp_scales = pack4(np.random.standard_normal((D, H)) / np.sqrt(D) / s[:, None] * t)
    wz = bf(np.random.standard_normal((Z, H)) / np.sqrt(Z) * t)
    b = bf(0.3 * np.random.standard_normal(H) * t)
    w2_words, w2_scales = pack4(np.random.standard_normal((H, CZ)) / np.sqrt(H) / t[:, None])
    wb_words, wb_scales = pack4(np.random.standard_normal((D, C)) / np.sqrt(D) / s[:, None])
    return {
        "phi": phi,
        "z": z,
        "wp_words": wp_words,
        "wp_scales": wp_scales,
        "wz": wz,
        "b": b,
        "w2_words": w2_words,
        "w2_scales": w2_scales,
        "wb_words": wb_words,
        "wb_scales": wb_scales,
    }


def core(phi, z, wp_words, wp_scales, wz, b, w2_words, w2_scales, wb_words, wb_scales):
    z = f64(z)
    n, zdim = z.shape
    c = wb_scales.shape[2]
    phiq = mxq(f64(phi), 1, "e4m3")
    q = index_hidden(phiq, z, unpack4(wp_words, wp_scales), f64(wz), f64(b))
    sigma = (mxq(q, 1, "e4m3") @ unpack4(w2_words, w2_scales)).reshape(n, c, zdim)
    epi = np.sum(sigma * z[:, None, :], axis=-1) / np.sqrt(zdim)
    base = phiq @ unpack4(wb_words, wb_scales)
    return base + epi


def setup_inputs():
    drawn = draw0()
    full = np.asarray(drawn['phi']).astype(np.float64)
    scale = (np.abs(full).reshape(4, 128, 8, 128).max(axis=(1, 3)) / 448.0).astype(np.float32)
    given = {}
    for key, value in drawn.items():
        if key == 'phi':
            given['phi_bytes'] = e4m3fn_bytes(full / np.repeat(np.repeat(scale.astype(np.float64), 128, axis=0), 128, axis=1))
            given['phi_scale'] = scale
        else:
            given[key] = value
    return given


def reference(phi_bytes, phi_scale, z, wp_words, wp_scales, wz, b, w2_words, w2_scales, wb_words, wb_scales):
    return core(e4m3fn_values(phi_bytes) * np.repeat(np.repeat(phi_scale.astype(np.float64), 128, axis=0), 128, axis=1), z, wp_words, wp_scales, wz, b, w2_words, w2_scales, wb_words, wb_scales)

@@ -1,0 +1,387 @@
+import math
+from contextlib import ExitStack
+
+import concourse.mybir as mybir
+from concourse.masks import make_identity
+
+N, D, H, Z, C = 512, 1024, 512, 128, 128
+FLOPS = 2 * N * D * H + 2 * N * Z * H + 2 * N * H * C * Z + 2 * N * C * Z + 2 * N * D * C
+
+F32 = mybir.dt.float32
+BF16 = mybir.dt.bfloat16
+I32 = mybir.dt.int32
+U32 = mybir.dt.uint32
+U8 = mybir.dt.uint8
+FP8 = mybir.dt.float8_e4m3fn
+FP8X4 = mybir.dt.float8_e4m3fn_x4
+FP4X4 = mybir.dt.float4_e2m1fn_x4
+ADD = mybir.AluOpType.add
+MULT = mybir.AluOpType.mult
+ACT = mybir.ActivationFunctionType
+
+P = 128
+ROWS = N // P
+KI = 4
+KC = Z // KI
+QUARTERS = 4
+CQ = C // QUARTERS
+
+SH_A = (11, 6)
+SH_B = (6, 6)
+SH_F = (12, 8)
+GACC = 2
+RUN = 4
+LAG = 6
+FIN = (5, 5, 10, 11)
+PERM_POS = (7, 12, 13)
+HID_POS = (8, 12, 24)
+QP_POS = (1, 4, 12)
+BASE_POS = 16
+WIDEN_ON = "VVSS"
+
+
+def tile_epinetindexedattributerewards_d2p_kernel(
+    tc, phi_bytes, phi_scale, z, wp_words, wp_scales, wz, b, w2_words, w2_scales, wb_words, wb_scales, out
+):
+    nc = tc.nc
+    with ExitStack() as ctx:
+        keep = ctx.enter_context(tc.tile_pool(name="keep", bufs=1))
+        prods = ctx.enter_context(tc.tile_pool(name="prods", bufs=16))
+        small = ctx.enter_context(tc.tile_pool(name="small", bufs=2))
+        ring = ctx.enter_context(tc.psum_pool(name="ring", bufs=7))
+        tacc = ctx.enter_context(tc.psum_pool(name="tacc", bufs=1))
+        ctx.enter_context(tc.manual_schedule())
+
+        ident = keep.tile([P, P], F32, name="ident", align_bytes=64)
+        ident_bf = keep.tile([P, P], BF16, name="ident_bf", align_bytes=64)
+        pscale = keep.tile([P, 32], F32, name="pscale")
+        z_bf = keep.tile([P, ROWS, Z], BF16, name="z_bf")
+        zs = keep.tile([P, ROWS, Z], F32, name="zs")
+        z_t = keep.tile([P, N], BF16, name="z_t")
+        wp_raw = keep.tile([P, 2 * 2 * H], U8, name="wp_raw", align_bytes=64)
+        wp_w = keep.tile([P, 2, 4, 256], U8, name="wp_w", align_bytes=64)
+        wps_raw = keep.tile([P, 2 * H], U8, name="wps_raw", align_bytes=64)
+        wp_s = keep.tile([P, 2, 4, P], U8, name="wp_s", align_bytes=64)
+        wz_sb = keep.tile([P, H], BF16, name="wz_sb", align_bytes=64)
+        b_sb = keep.tile([P, 4], BF16, name="b_sb")
+        wb_w = keep.tile([P, 2, 256], U8, name="wb_w", align_bytes=64)
+        wb_s = keep.tile([P, 2, C], U8, name="wb_s", align_bytes=64)
+        w2_s_raw = [keep.tile([P, C * Z // 2], U8, name=f"w2_s_raw{h}", align_bytes=64) for h in range(2)]
+        w2_s = keep.tile([P, KC, C * KI], U8, name="w2_s", align_bytes=64)
+        w2_w = keep.tile([P, KC, 2 * C * KI], U8, name="w2_w", align_bytes=64)
+        w2_raw = [keep.tile([P, 2 * CQ * Z], U8, name=f"w2_raw{q}", align_bytes=64) for q in range(QUARTERS)]
+        phib0 = keep.tile([P, D], U8, name="phib0", align_bytes=64)
+        phib_rest = keep.tile([P, ROWS - 1, D], U8, name="phib_rest", align_bytes=64)
+        phib = [phib0[:]] + [phib_rest[:, r, :] for r in range(ROWS - 1)]
+        phi_bf = [keep.tile([P, D], BF16, name=f"phi_bf{r}", align_bytes=64) for r in range(ROWS)]
+        phig = [keep.tile([P, 2, P, 4], BF16, name=f"phig{r}", align_bytes=64) for r in range(ROWS)]
+        phic = [keep.tile([P, 2 * P], U32, name=f"phic{r}", align_bytes=64) for r in range(ROWS)]
+        phis = [keep.tile([P, 2 * P], U8, name=f"phis{r}", align_bytes=64) for r in range(ROWS)]
+        zwb = keep.tile([P, 4, N], F32, name="zwb")
+        hsum = [keep.tile([P, 4, P], F32, name=f"hsum{r}") for r in range(ROWS)]
+        qg = [keep.tile([P, P, 4], BF16, name=f"qg{r}", align_bytes=64) for r in range(ROWS)]
+        qc = [keep.tile([P, P], U32, name=f"qc{r}", align_bytes=64) for r in range(ROWS)]
+        qs = [keep.tile([P, P], U8, name=f"qs{r}", align_bytes=64) for r in range(ROWS)]
+        base = keep.tile([P, ROWS, C], F32, name="base")
+        acc_v = [keep.tile([P, KI * C], F32, name=f"acc_v{a}") for a in range(ROWS + 1)]
+        acc_g = [[keep.tile([P, KI * C], F32, name=f"acc_g{a}_{e}") for e in range(GACC)] for a in range(ROWS + 1)]
+
+        nc.vector.memset(wps_raw[:].bitcast(I32), 0)
+        nc.vector.memset(w2_s_raw[0][:].bitcast(I32), 0)
+        nc.vector.memset(wb_s[:].rearrange("p g n -> p (g n)").bitcast(I32), 0)
+        nc.vector.memset(w2_s_raw[1][:].bitcast(I32), 0)
+        make_identity(nc, ident[:])
+        make_identity(nc, ident_bf[:])
+
+        nc.sync.dma_start(out=phib0[:], in_=phi_bytes[0:P, :])
+        nc.sync.dma_start(out=pscale[:], in_=phi_scale.rearrange("i j -> (i j)").partition_broadcast(P))
+        nc.sync.dma_start(
+            out=wp_raw[:].rearrange("p (g n) -> p g n", g=2).bitcast(I32),
+            in_=wp_words.rearrange("g p n -> p g n").bitcast(I32),
+        )
+        nc.sync.dma_start(out=z_bf[:], in_=z.rearrange("(r p) k -> p r k", p=P))
+        nc.sync.dma_start(out=wz_sb[:], in_=wz)
+        nc.sync.dma_start(out=b_sb[:], in_=b.rearrange("(p t) -> p t", t=4))
+        nc.sync.dma_start(out=phib_rest[:], in_=phi_bytes[P:, :].rearrange("(r p) k -> p r k", p=P))
+        for q in range(4):
+            nc.gpsimd.dma_start(
+                out=wps_raw[32 * q : 32 * q + 4, :].rearrange("p (g n) -> p g n", g=2).bitcast(I32),
+                in_=wp_scales[:, 4 * q : 4 * q + 4, :].rearrange("g q n -> q g n").bitcast(I32),
+            )
+        nc.gpsimd.tensor_scalar(zs[:], z_bf[:], 1.0 / math.sqrt(Z), 0.0, op0=MULT, op1=ADD)
+        for q in range(4):
+            nc.gpsimd.dma_start(
+                out=wb_s[32 * q : 32 * q + 4, :, :].bitcast(I32),
+                in_=wb_scales[:, 4 * q : 4 * q + 4, :].rearrange("g q n -> q g n").bitcast(I32),
+            )
+        half = C * Z // 2
+        for h in range(2):
+            for q in range(4):
+                nc.sync.dma_start(
+                    out=w2_s_raw[h][32 * q : 32 * q + 4, :].bitcast(I32),
+                    in_=w2_scales[0, 4 * q : 4 * q + 4, h * half : (h + 1) * half].bitcast(I32),
+                )
+            for q in (2 * h, 2 * h + 1):
+                width = 2 * CQ * Z
+                nc.sync.dma_start(
+                    out=w2_raw[q][:].bitcast(I32), in_=w2_words[0, :, q * width : (q + 1) * width].bitcast(I32)
+                )
+            if h == 0:
+                nc.sync.dma_start(out=wb_w[:].bitcast(I32), in_=wb_words.rearrange("g p n -> p g n").bitcast(I32))
+
+        w2_s_i = w2_s[:].rearrange("p k n -> p (k n)").bitcast(I32).rearrange("p (k c) -> p k c", k=KC)
+        w2_w_i = w2_w[:].rearrange("p k n -> p (k n)").bitcast(I32).rearrange("p (k c w) -> p k c w", k=KC, w=2)
+
+        def permute_scales(h):
+            nc.vector.tensor_copy(
+                out=w2_s_i[:, :, h * C // 2 : (h + 1) * C // 2],
+                in_=w2_s_raw[h][:].bitcast(I32).rearrange("p (c k) -> p k c", k=KC),
+            )
+
+        def permute_words(q):
+            nc.vector.tensor_copy(
+                out=w2_w_i[:, :, q * CQ : (q + 1) * CQ, :],
+                in_=w2_raw[q][:].bitcast(I32).rearrange("p (c k w) -> p k c w", k=KC, w=2),
+            )
+
+        def widen(r):
+            for j in range(D // P):
+                cols = slice(j * P, (j + 1) * P)
+                src = phib[r][:, cols].bitcast(FP8)
+                factor = pscale[:, 8 * r + j : 8 * r + j + 1]
+                if WIDEN_ON[r] == "V":
+                    nc.vector.tensor_scalar(phi_bf[r][:, cols], src, factor, None, op0=MULT)
+                else:
+                    nc.scalar.activation(phi_bf[r][:, cols], src, ACT.Copy, scale=factor)
+
+        def turn(r):
+            bank = ring.tile([P, 2, 2, P], F32, name="bank")
+            words = phi_bf[r][:].bitcast(F32)
+            for g in range(2):
+                for u in range(2):
+                    nc.tensor.transpose(bank[:, g, u, :], words[:, 256 * g + u : 256 * (g + 1) : 2], ident[:])
+            for g in range(2):
+                nc.scalar.copy(
+                    phig[r][:, g, :, :].rearrange("p n j -> p (n j)").bitcast(F32).rearrange("p (n u) -> p n u", u=2),
+                    bank[:, g, :, :].rearrange("p u n -> p n u"),
+                )
+
+        def quantize_phi(r):
+            nc.vector.quantize_mx(
+                out=phic[r][:].bitcast(FP8X4), scales=phis[r][:], in_=phig[r][:].rearrange("p g n j -> p (g n j)")
+            )
+
+        hbanks = {}
+
+        def hidden_mm(r):
+            bank = ring.tile([P, 4, P], F32, name="bank")
+            hbanks[r] = bank
+            for t in range(4):
+                for g in range(2):
+                    nc.tensor.matmul_mx(
+                        out=bank[:, t, :],
+                        lhsT=wp_w[:, g, t, :].bitcast(FP4X4),
+                        lhsT_scale=wp_s[:, g, t, :],
+                        rhs=phic[r][:, g * P : (g + 1) * P].bitcast(FP8X4),
+                        rhs_scale=phis[r][:, g * P : (g + 1) * P],
+                        start=(g == 0),
+                        stop=(g == 1),
+                    )
+
+        def hidden_add(r):
+            nc.vector.tensor_tensor(out=hsum[r][:], in0=hbanks[r][:], in1=zwb[:, :, r * P : (r + 1) * P], op=ADD)
+
+        def hidden_relu(r):
+            nc.scalar.activation(qg[r][:], hsum[r][:].rearrange("p t n -> p n t"), ACT.Relu)
+
+        def quantize_q(r):
+            nc.vector.quantize_mx(out=qc[r][:].bitcast(FP8X4), scales=qs[r][:], in_=qg[r][:].rearrange("p n t -> p (n t)"))
+
+        widen(0)
+        turn(0)
+        for g in range(2):
+            nc.vector.tensor_copy(
+                out=wp_w[:, g, :, :].rearrange("p t (m b) -> p t m b", b=2),
+                in_=wp_raw[:, g * 1024 : (g + 1) * 1024].rearrange("p (m t b) -> p t m b", t=4, b=2),
+            )
+        quantize_phi(0)
+        for g in range(2):
+            nc.vector.tensor_copy(
+                out=wp_s[:, g, :, :], in_=wps_raw[:, g * H : (g + 1) * H].rearrange("p (m t) -> p t m", t=4)
+            )
+        zbank = ring.tile([P, N], BF16, name="bank")
+        for r in range(ROWS):
+            nc.tensor.transpose(zbank[:, r * P : (r + 1) * P], z_bf[:, r, :], ident_bf[:])
+        nc.scalar.copy(z_t[:], zbank[:])
+        wz_t = wz_sb[:].rearrange("z (m t) -> z t m", t=4)
+        for t in range(4):
+            bank = ring.tile([P, N], F32, name="bank")
+            nc.tensor.matmul(bank[:], lhsT=wz_t[:, t, :], rhs=z_t[:], start=True, stop=True)
+            nc.scalar.activation(zwb[:, t, :], bank[:], ACT.Identity, bias=b_sb[:, t : t + 1])
+        hidden_mm(0)
+        widen(1)
+        hidden_add(0)
+        hidden_relu(0)
+        permute_scales(0)
+        quantize_q(0)
+        turn(1)
+        for r in range(2, ROWS):
+            widen(r)
+            turn(r)
+        permute_words(0)
+        permute_words(1)
+
+        def pattern(count, n_scalar, n_gpsimd):
+            share = ["S" if (i + 1) * n_scalar // count > i * n_scalar // count else "V" for i in range(count)]
+            seen = 0
+            for i in range(count):
+                if share[i] == "S":
+                    if (seen + 1) * n_gpsimd // n_scalar > seen * n_gpsimd // n_scalar:
+                        share[i] = "G"
+                    seen += 1
+            return share
+
+        jobs = []
+        for a, sh in ((0, SH_A), (1, SH_B)):
+            jobs += [(a, 0, 2 * i, who, a) for i, who in enumerate(pattern(KC // 2, *sh))]
+        for r in range(1, ROWS):
+            jobs += [(r + 1, r, i, who, None) for i, who in enumerate(pattern(KC, *SH_F))]
+
+        events = {}
+
+        def at(pos, f):
+            events.setdefault(pos, []).append(f)
+
+        sums = [{"first": True, "tile": None, "v": 0, "g": 0, "held": [], "run": []} for a in range(ROWS + 1)]
+
+        def turn_sum(a, pieces, last):
+            st = sums[a]
+            if st["tile"] is None:
+                acc_t = tacc.tile([P, P], F32, name="acc_t")
+                st["tile"] = acc_t
+            for n, piece in enumerate(pieces):
+                nc.tensor.matmul(
+                    st["tile"][:], lhsT=piece, rhs=ident[:], is_transpose=True, start=st["first"], stop=(last and n == len(pieces) - 1)
+                )
+                st["first"] = False
+
+        def quads(t):
+            return [t[:, n * C : (n + 1) * C] for n in range(KI)]
+
+        def finish(pos, a, r, half):
+            acc_s = small.tile([P, P], F32, name="acc_s")
+            st = sums[a]
+
+            def step0():
+                turn_sum(a, quads(acc_v[a]) + [p for e in range(min(GACC, st["g"] // 2)) for p in quads(acc_g[a][e])], True)
+
+            def step1():
+                nc.scalar.copy(acc_s[:], st["tile"][:])
+
+            def step2():
+                back = ring.tile([P, P], F32, name="bank")
+                st["back"] = back
+                nc.tensor.transpose(back[:], acc_s[:], ident[:])
+
+            def step3():
+                back = st["back"]
+                if half is None:
+                    res = small.tile([P, C], F32, name="res")
+                    nc.vector.tensor_tensor(out=res[:], in0=back[:], in1=base[:, r, :], op=ADD)
+                    nc.sync.dma_start(out=out[r * P : (r + 1) * P, :], in_=res[:])
+                else:
+                    cols = slice(half * C // 2, (half + 1) * C // 2)
+                    part = small.tile([P, C // 2], F32, name="part")
+                    hres = small.tile([P, C // 2], F32, name="hres")
+                    nc.vector.tensor_tensor(out=part[:], in0=back[:, 0 : C // 2], in1=base[:, r, cols], op=ADD)
+                    nc.vector.tensor_tensor(out=hres[:], in0=back[:, C // 2 : C], in1=part[:], op=ADD)
+                    nc.sync.dma_start(out=out[r * P : (r + 1) * P, cols], in_=hres[:])
+
+            for lag, f in zip(FIN, (step0, step1, step2, step3)):
+                at(pos + lag, f)
+
+        def base_rows():
+            bbank = ring.tile([P, ROWS, C], F32, name="bank")
+            for r in range(ROWS):
+                for g in range(2):
+                    nc.tensor.matmul_mx(
+                        out=bbank[:, r, :],
+                        lhsT=phic[r][:, g * P : (g + 1) * P].bitcast(FP8X4),
+                        lhsT_scale=phis[r][:, g * P : (g + 1) * P],
+                        rhs=wb_w[:, g, :].bitcast(FP4X4),
+                        rhs_scale=wb_s[:, g, :],
+                        start=(g == 0),
+                        stop=(g == 1),
+                    )
+            nc.scalar.copy(base[:], bbank[:])
+
+        at(PERM_POS[0], lambda: permute_scales(1))
+        at(PERM_POS[1], lambda: permute_words(2))
+        at(PERM_POS[2], lambda: permute_words(3))
+        at(BASE_POS, base_rows)
+        for r in range(1, ROWS):
+            at(QP_POS[r - 1], lambda r=r: quantize_phi(r))
+            at(HID_POS[r - 1], lambda r=r: hidden_mm(r))
+            at(HID_POS[r - 1] + 3, lambda r=r: hidden_add(r))
+            at(HID_POS[r - 1] + 5, lambda r=r: hidden_relu(r))
+            at(HID_POS[r - 1] + 9, lambda r=r: quantize_q(r))
+
+        for pos, (a, r, chunk, who, half) in enumerate(jobs):
+            for f in events.pop(pos, []):
+                f()
+            st = sums[a]
+            bank = ring.tile([P, C * KI], F32, name="bank")
+            if half is None:
+                spans = [(chunk, slice(0, 512), slice(0, 512))]
+                cols = bank[:].rearrange("p (c k) -> p k c", k=KI)
+                parts = [(KI * chunk + k, cols[:, k, :]) for k in range(KI)]
+            else:
+                spans = [(chunk + e, slice(256 * e, 256 * e + 256), slice(256 * half, 256 * half + 256)) for e in range(2)]
+                cols = bank[:].rearrange("p (e c k) -> p e k c", e=2, k=KI)
+                parts = [(KI * (chunk + e) + k, cols[:, e, k, :]) for e in range(2) for k in range(KI)]
+            for kc, dst, src in spans:
+                nc.tensor.matmul_mx(
+                    out=bank[:, dst],
+                    lhsT=qc[r][:].bitcast(FP8X4),
+                    lhsT_scale=qs[r][:],
+                    rhs=w2_w[:, kc, 2 * src.start : 2 * src.stop].bitcast(FP4X4),
+                    rhs_scale=w2_s[:, kc, src],
+                    start=True,
+                    stop=True,
+                )
+            width = 512 // len(parts)
+            if who == "V":
+                for n, (k, col) in enumerate(parts):
+                    dst = acc_v[a][:, n * width : (n + 1) * width]
+                    zk = zs[:, r, k : k + 1]
+                    if st["v"] == 0:
+                        nc.vector.tensor_scalar(dst, col, zk, None, op0=MULT)
+                    else:
+                        nc.vector.scalar_tensor_tensor(out=dst, in0=col, scalar=zk, in1=dst, op0=MULT, op1=ADD)
+                st["v"] += 1
+            else:
+                prod = prods.tile([P, C * KI], F32, name="prod")
+                for n, (k, col) in enumerate(parts):
+                    nc.scalar.activation(prod[:, n * width : (n + 1) * width], col, ACT.Copy, scale=zs[:, r, k : k + 1])
+                if who == "G":
+                    e = st["g"] // 2 if st["g"] < 2 * GACC else st["g"] % GACC
+                    if st["g"] < 2 * GACC and st["g"] % 2 == 0:
+                        st["held"] = [prod]
+                    else:
+                        first = st["held"].pop() if st["g"] < 2 * GACC else acc_g[a][e]
+                        nc.gpsimd.tensor_tensor(out=acc_g[a][e][:], in0=first[:], in1=prod[:], op=ADD)
+                    st["g"] += 1
+                else:
+                    st["run"].append(prod)
+            done = pos + 1 == len(jobs) or jobs[pos + 1][0] != a
+            if len(st["run"]) == RUN or (done and st["run"]):
+                pieces = [p for t in st["run"] for p in quads(t)]
+                at(pos + LAG, lambda pieces=pieces, a=a: turn_sum(a, pieces, False))
+                st["run"] = []
+            if done:
+                if st["held"]:
+                    at(pos + LAG, lambda pieces=quads(st["held"][0]), a=a: turn_sum(a, pieces, False))
+                finish(pos + LAG, a, r, half)
+        for pos in sorted(events):
+            for f in events[pos]:
+                f()

@@ -17,6 +17,7 @@ FP8X4 = mybir.dt.float8_e4m3fn_x4
 FP4X4 = mybir.dt.float4_e2m1fn_x4
 ADD = mybir.AluOpType.add
 MULT = mybir.AluOpType.mult
+MAX = mybir.AluOpType.max
 ACT = mybir.ActivationFunctionType
 
 P = 128
@@ -26,18 +27,21 @@ KC = Z // KI
 QUARTERS = 4
 CQ = C // QUARTERS
 
-SH_A = (11, 6)
+SH_A = (9, 9)
 SH_B = (6, 6)
 SH_F = (12, 8)
 GACC = 2
 RUN = 4
-LAG = 6
-FIN = (5, 5, 10, 11)
-PERM_POS = (7, 12, 13)
-HID_POS = (8, 12, 24)
-QP_POS = (1, 4, 12)
-BASE_POS = 16
-WIDEN_ON = "VVSS"
+LAG = 8
+FIN = (5, 6, 10, 11)
+SH_L = (13, 8, 9)
+RELU_ON = "SSGG"
+AHEAD = 4
+WID_POS = (6, 32, 65)
+PERM_POS = (5, 7, 11)
+STEPS = (0, 2, 3, 4, 3, 1, 5, 1)
+BASE_POS = 10
+WIDEN_ON = "VSVS"
 
 
 def tile_epinetindexedattributerewards_d2p_kernel(
@@ -83,7 +87,7 @@ def tile_epinetindexedattributerewards_d2p_kernel(
         qc = [keep.tile([P, P], U32, name=f"qc{r}", align_bytes=64) for r in range(ROWS)]
         qs = [keep.tile([P, P], U8, name=f"qs{r}", align_bytes=64) for r in range(ROWS)]
         base = keep.tile([P, ROWS, C], F32, name="base")
-        acc_v = [keep.tile([P, KI * C], F32, name=f"acc_v{a}") for a in range(ROWS + 1)]
+        acc_v = [[keep.tile([P, KI * C], F32, name=f"acc_v{a}_{e}") for e in range(2)] for a in range(ROWS + 1)]
         acc_g = [[keep.tile([P, KI * C], F32, name=f"acc_g{a}_{e}") for e in range(GACC)] for a in range(ROWS + 1)]
 
         nc.vector.memset(wps_raw[:].bitcast(I32), 0)
@@ -102,7 +106,6 @@ def tile_epinetindexedattributerewards_d2p_kernel(
         nc.sync.dma_start(out=z_bf[:], in_=z.rearrange("(r p) k -> p r k", p=P))
         nc.sync.dma_start(out=wz_sb[:], in_=wz)
         nc.sync.dma_start(out=b_sb[:], in_=b.rearrange("(p t) -> p t", t=4))
-        nc.sync.dma_start(out=phib_rest[:], in_=phi_bytes[P:, :].rearrange("(r p) k -> p r k", p=P))
         for q in range(4):
             nc.gpsimd.dma_start(
                 out=wps_raw[32 * q : 32 * q + 4, :].rearrange("p (g n) -> p g n", g=2).bitcast(I32),
@@ -127,6 +130,7 @@ def tile_epinetindexedattributerewards_d2p_kernel(
                     out=w2_raw[q][:].bitcast(I32), in_=w2_words[0, :, q * width : (q + 1) * width].bitcast(I32)
                 )
             if h == 0:
+                nc.sync.dma_start(out=phib_rest[:], in_=phi_bytes[P:, :].rearrange("(r p) k -> p r k", p=P))
                 nc.sync.dma_start(out=wb_w[:].bitcast(I32), in_=wb_words.rearrange("g p n -> p g n").bitcast(I32))
 
         w2_s_i = w2_s[:].rearrange("p k n -> p (k n)").bitcast(I32).rearrange("p (k c) -> p k c", k=KC)
@@ -192,7 +196,10 @@ def tile_epinetindexedattributerewards_d2p_kernel(
             nc.vector.tensor_tensor(out=hsum[r][:], in0=hbanks[r][:], in1=zwb[:, :, r * P : (r + 1) * P], op=ADD)
 
         def hidden_relu(r):
-            nc.scalar.activation(qg[r][:], hsum[r][:].rearrange("p t n -> p n t"), ACT.Relu)
+            if RELU_ON[r] == "S":
+                nc.scalar.activation(qg[r][:], hsum[r][:].rearrange("p t n -> p n t"), ACT.Relu)
+            else:
+                nc.gpsimd.tensor_scalar(qg[r][:], hsum[r][:].rearrange("p t n -> p n t"), 0.0, 0.0, op0=MAX, op1=ADD)
 
         def quantize_q(r):
             nc.vector.quantize_mx(out=qc[r][:].bitcast(FP8X4), scales=qs[r][:], in_=qg[r][:].rearrange("p n t -> p (n t)"))
@@ -219,40 +226,37 @@ def tile_epinetindexedattributerewards_d2p_kernel(
             nc.tensor.matmul(bank[:], lhsT=wz_t[:, t, :], rhs=z_t[:], start=True, stop=True)
             nc.scalar.activation(zwb[:, t, :], bank[:], ACT.Identity, bias=b_sb[:, t : t + 1])
         hidden_mm(0)
-        widen(1)
+        permute_scales(0)
         hidden_add(0)
         hidden_relu(0)
-        permute_scales(0)
-        quantize_q(0)
-        turn(1)
-        for r in range(2, ROWS):
-            widen(r)
-            turn(r)
         permute_words(0)
+        quantize_q(0)
         permute_words(1)
 
-        def pattern(count, n_scalar, n_gpsimd):
-            share = ["S" if (i + 1) * n_scalar // count > i * n_scalar // count else "V" for i in range(count)]
-            seen = 0
-            for i in range(count):
-                if share[i] == "S":
-                    if (seen + 1) * n_gpsimd // n_scalar > seen * n_gpsimd // n_scalar:
-                        share[i] = "G"
-                    seen += 1
+        def pattern(rest, n_scalar, n_gpsimd, tail):
+            share = ["S" if (i + 1) * n_scalar // rest > i * n_scalar // rest else "V" for i in range(rest)]
+            early = [i for i in range(rest - tail) if share[i] == "S"]
+            for n, i in enumerate(early):
+                if (n + 1) * n_gpsimd // len(early) > n * n_gpsimd // len(early):
+                    share[i] = "G"
             return share
 
         jobs = []
         for a, sh in ((0, SH_A), (1, SH_B)):
-            jobs += [(a, 0, 2 * i, who, a) for i, who in enumerate(pattern(KC // 2, *sh))]
+            jobs += [(a, 0, 2 * i, who, a) for i, who in enumerate(pattern(KC // 2, *sh, 0))]
         for r in range(1, ROWS):
-            jobs += [(r + 1, r, i, who, None) for i, who in enumerate(pattern(KC, *SH_F))]
+            sh = SH_L if r == ROWS - 1 else (*SH_F, 0)
+            jobs.insert(len(jobs) - AHEAD, (r + 1, r, 0, "A", None))
+            jobs.insert(len(jobs) - AHEAD + 2, (r + 1, r, 1, "A", None))
+            jobs += [(r + 1, r, i + 2, who, None) for i, who in enumerate(pattern(KC - 2, *sh))]
+        last_job = {job[0]: pos for pos, job in enumerate(jobs)}
 
         events = {}
 
         def at(pos, f):
             events.setdefault(pos, []).append(f)
 
-        sums = [{"first": True, "tile": None, "v": 0, "g": 0, "held": [], "run": []} for a in range(ROWS + 1)]
+        sums = [{"first": True, "tile": None, "v": 0, "g": 0, "held": [], "run": [], "init": []} for a in range(ROWS + 1)]
 
         def turn_sum(a, pieces, last):
             st = sums[a]
@@ -273,7 +277,7 @@ def tile_epinetindexedattributerewards_d2p_kernel(
             st = sums[a]
 
             def step0():
-                turn_sum(a, quads(acc_v[a]) + [p for e in range(min(GACC, st["g"] // 2)) for p in quads(acc_g[a][e])], True)
+                turn_sum(a, quads(acc_v[a][0]) + quads(acc_v[a][1]) + [p for e in range(min(GACC, st["g"] // 2)) for p in quads(acc_g[a][e])], True)
 
             def step1():
                 nc.scalar.copy(acc_s[:], st["tile"][:])
@@ -300,31 +304,31 @@ def tile_epinetindexedattributerewards_d2p_kernel(
             for lag, f in zip(FIN, (step0, step1, step2, step3)):
                 at(pos + lag, f)
 
-        def base_rows():
-            bbank = ring.tile([P, ROWS, C], F32, name="bank")
-            for r in range(ROWS):
-                for g in range(2):
-                    nc.tensor.matmul_mx(
-                        out=bbank[:, r, :],
-                        lhsT=phic[r][:, g * P : (g + 1) * P].bitcast(FP8X4),
-                        lhsT_scale=phis[r][:, g * P : (g + 1) * P],
-                        rhs=wb_w[:, g, :].bitcast(FP4X4),
-                        rhs_scale=wb_s[:, g, :],
-                        start=(g == 0),
-                        stop=(g == 1),
-                    )
-            nc.scalar.copy(base[:], bbank[:])
+        def base_rows(r):
+            bbank = ring.tile([P, C], F32, name="bank")
+            for g in range(2):
+                nc.tensor.matmul_mx(
+                    out=bbank[:],
+                    lhsT=phic[r][:, g * P : (g + 1) * P].bitcast(FP8X4),
+                    lhsT_scale=phis[r][:, g * P : (g + 1) * P],
+                    rhs=wb_w[:, g, :].bitcast(FP4X4),
+                    rhs_scale=wb_s[:, g, :],
+                    start=(g == 0),
+                    stop=(g == 1),
+                )
+            nc.scalar.copy(base[:, r, :], bbank[:])
+
 
         at(PERM_POS[0], lambda: permute_scales(1))
         at(PERM_POS[1], lambda: permute_words(2))
         at(PERM_POS[2], lambda: permute_words(3))
-        at(BASE_POS, base_rows)
+        at(BASE_POS, lambda: base_rows(0))
         for r in range(1, ROWS):
-            at(QP_POS[r - 1], lambda r=r: quantize_phi(r))
-            at(HID_POS[r - 1], lambda r=r: hidden_mm(r))
-            at(HID_POS[r - 1] + 3, lambda r=r: hidden_add(r))
-            at(HID_POS[r - 1] + 5, lambda r=r: hidden_relu(r))
-            at(HID_POS[r - 1] + 9, lambda r=r: quantize_q(r))
+            chain = (widen, turn, quantize_phi, hidden_mm, hidden_add, hidden_relu, quantize_q, base_rows)
+            pos = WID_POS[r - 1]
+            for step, f in zip(STEPS, chain):
+                pos += step
+                at(pos, lambda r=r, f=f: f(r))
 
         for pos, (a, r, chunk, who, half) in enumerate(jobs):
             for f in events.pop(pos, []):
@@ -351,19 +355,25 @@ def tile_epinetindexedattributerewards_d2p_kernel(
                 )
             width = 512 // len(parts)
             if who == "V":
-                for n, (k, col) in enumerate(parts):
-                    dst = acc_v[a][:, n * width : (n + 1) * width]
+                order = list(enumerate(parts))
+                if st["v"] // 2 % 2:
+                    order.reverse()
+                for n, (k, col) in order:
+                    dst = acc_v[a][st["v"] % 2][:, n * width : (n + 1) * width]
                     zk = zs[:, r, k : k + 1]
-                    if st["v"] == 0:
+                    if st["v"] < 2 and not st["init"]:
                         nc.vector.tensor_scalar(dst, col, zk, None, op0=MULT)
-                    else:
-                        nc.vector.scalar_tensor_tensor(out=dst, in0=col, scalar=zk, in1=dst, op0=MULT, op1=ADD)
+                        continue
+                    prior = dst if st["v"] >= 2 else st["init"][st["v"]][:, n * width : (n + 1) * width]
+                    nc.vector.scalar_tensor_tensor(out=dst, in0=col, scalar=zk, in1=prior, op0=MULT, op1=ADD)
                 st["v"] += 1
             else:
                 prod = prods.tile([P, C * KI], F32, name="prod")
                 for n, (k, col) in enumerate(parts):
                     nc.scalar.activation(prod[:, n * width : (n + 1) * width], col, ACT.Copy, scale=zs[:, r, k : k + 1])
-                if who == "G":
+                if who == "A":
+                    st["init"].append(prod)
+                elif who == "G":
                     e = st["g"] // 2 if st["g"] < 2 * GACC else st["g"] % GACC
                     if st["g"] < 2 * GACC and st["g"] % 2 == 0:
                         st["held"] = [prod]
@@ -373,7 +383,7 @@ def tile_epinetindexedattributerewards_d2p_kernel(
                     st["g"] += 1
                 else:
                     st["run"].append(prod)
-            done = pos + 1 == len(jobs) or jobs[pos + 1][0] != a
+            done = pos == last_job[a]
             if len(st["run"]) == RUN or (done and st["run"]):
                 pieces = [p for t in st["run"] for p in quads(t)]
                 at(pos + LAG, lambda pieces=pieces, a=a: turn_sum(a, pieces, False))

@@ -27,20 +27,20 @@ KC = Z // KI
 QUARTERS = 4
 CQ = C // QUARTERS
 
-SH_A = (9, 9)
-SH_B = (6, 6)
-SH_F = (12, 8)
+SH_A = (9, 0)
+SH_B = (5, 0)
+SH_F = (8, 0)
 GACC = 2
-RUN = 4
-LAG = 8
-FIN = (5, 6, 10, 11)
-SH_L = (13, 8, 9)
-RELU_ON = "SSGG"
-AHEAD = 4
-WID_POS = (6, 32, 65)
-PERM_POS = (5, 7, 11)
-STEPS = (0, 2, 3, 4, 3, 1, 5, 1)
-BASE_POS = 10
+RUN = 3
+LAG = 6
+FIN = (6, 6, 10, 11)
+SH_L = (9, 0, 8)
+RELU_ON = "SSSS"
+AHEAD = 3
+WID_POS = (5, 31, 61)
+PERM_POS = (5, 9, 11)
+STEPS = (0, 3, 2, 4, 2, 4, 5, 3)
+BASE_POS = 8
 WIDEN_ON = "VSVS"
 
 
@@ -277,7 +277,7 @@ def tile_epinetindexedattributerewards_d2p_kernel(
             st = sums[a]
 
             def step0():
-                turn_sum(a, quads(acc_v[a][0]) + quads(acc_v[a][1]) + [p for e in range(min(GACC, st["g"] // 2)) for p in quads(acc_g[a][e])], True)
+                turn_sum(a, [p for e in range(min(GACC, st["g"] // 2)) for p in quads(acc_g[a][e])] + quads(acc_v[a][st["v"] % 2]) + quads(acc_v[a][1 - st["v"] % 2]), True)
 
             def step1():
                 nc.scalar.copy(acc_s[:], st["tile"][:])
@@ -386,7 +386,8 @@ def tile_epinetindexedattributerewards_d2p_kernel(
             done = pos == last_job[a]
             if len(st["run"]) == RUN or (done and st["run"]):
                 pieces = [p for t in st["run"] for p in quads(t)]
-                at(pos + LAG, lambda pieces=pieces, a=a: turn_sum(a, pieces, False))
+                free_at = last_job[a - 1] + LAG + FIN[1] if a else 0
+                at(max(pos + LAG, free_at), lambda pieces=pieces, a=a: turn_sum(a, pieces, False))
                 st["run"] = []
             if done:
                 if st["held"]:

@@ -27,21 +27,25 @@ KC = Z // KI
 QUARTERS = 4
 CQ = C // QUARTERS
 
-SH_A = (9, 0)
-SH_B = (5, 0)
-SH_F = (8, 0)
-GACC = 2
+SH_A = (7, 8, 7)
+SH_B = (5, 6, 5)
+SH_F = (0, 13, 8)
+GACC = 1
 RUN = 3
 LAG = 6
-FIN = (6, 6, 10, 11)
-SH_L = (9, 0, 8)
+FIN = (11, 11, 13, 16)
+SH_L = (0, 13, 6, 7)
 RELU_ON = "SSSS"
-AHEAD = 3
-WID_POS = (5, 31, 61)
-PERM_POS = (5, 9, 11)
-STEPS = (0, 3, 2, 4, 2, 4, 5, 3)
-BASE_POS = 8
-WIDEN_ON = "VSVS"
+NSET = 1
+GAP = 6
+GW = 1
+TACC = 1
+AHEAD = 7
+WID_POS = (0, 34, 68)
+PERM_POS = (4, 9, 14)
+STEPS = (0, 7, 2, 5, 1, 2, 2, 5)
+BASE_POS = 12
+WIDEN_ON = "VVSS"
 
 
 def tile_epinetindexedattributerewards_d2p_kernel(
@@ -51,9 +55,10 @@ def tile_epinetindexedattributerewards_d2p_kernel(
     with ExitStack() as ctx:
         keep = ctx.enter_context(tc.tile_pool(name="keep", bufs=1))
         prods = ctx.enter_context(tc.tile_pool(name="prods", bufs=16))
+        pairs = ctx.enter_context(tc.tile_pool(name="pairs", bufs=6))
         small = ctx.enter_context(tc.tile_pool(name="small", bufs=2))
-        ring = ctx.enter_context(tc.psum_pool(name="ring", bufs=7))
-        tacc = ctx.enter_context(tc.psum_pool(name="tacc", bufs=1))
+        ring = ctx.enter_context(tc.psum_pool(name="ring", bufs=8 - TACC))
+        tacc = ctx.enter_context(tc.psum_pool(name="tacc", bufs=TACC))
         ctx.enter_context(tc.manual_schedule())
 
         ident = keep.tile([P, P], F32, name="ident", align_bytes=64)
@@ -68,8 +73,10 @@ def tile_epinetindexedattributerewards_d2p_kernel(
         wp_s = keep.tile([P, 2, 4, P], U8, name="wp_s", align_bytes=64)
         wz_sb = keep.tile([P, H], BF16, name="wz_sb", align_bytes=64)
         b_sb = keep.tile([P, 4], BF16, name="b_sb")
+        ones = keep.tile([P, P], F32, name="ones", align_bytes=64)
+        pscale_row = keep.tile([P, 32], F32, name="pscale_row", align_bytes=64)
         wb_w = keep.tile([P, 2, 256], U8, name="wb_w", align_bytes=64)
-        wb_s = keep.tile([P, 2, C], U8, name="wb_s", align_bytes=64)
+        wb_s = keep.tile([P, 2 * C], U8, name="wb_s", align_bytes=64)
         w2_s_raw = [keep.tile([P, C * Z // 2], U8, name=f"w2_s_raw{h}", align_bytes=64) for h in range(2)]
         w2_s = keep.tile([P, KC, C * KI], U8, name="w2_s", align_bytes=64)
         w2_w = keep.tile([P, KC, 2 * C * KI], U8, name="w2_w", align_bytes=64)
@@ -88,58 +95,63 @@ def tile_epinetindexedattributerewards_d2p_kernel(
         qs = [keep.tile([P, P], U8, name=f"qs{r}", align_bytes=64) for r in range(ROWS)]
         base = keep.tile([P, ROWS, C], F32, name="base")
         acc_v = [[keep.tile([P, KI * C], F32, name=f"acc_v{a}_{e}") for e in range(2)] for a in range(ROWS + 1)]
-        acc_g = [[keep.tile([P, KI * C], F32, name=f"acc_g{a}_{e}") for e in range(GACC)] for a in range(ROWS + 1)]
+        acc_g = [[keep.tile([P, GW * KI * C], F32, name=f"acc_g{a}_{e}") for e in range(GACC)] for a in range(ROWS + 1)]
 
-        nc.vector.memset(wps_raw[:].bitcast(I32), 0)
+        nc.vector.memset(pscale_row[:], 0.0)
+        nc.gpsimd.memset(ones[:], 1.0)
         nc.vector.memset(w2_s_raw[0][:].bitcast(I32), 0)
-        nc.vector.memset(wb_s[:].rearrange("p g n -> p (g n)").bitcast(I32), 0)
+        nc.vector.memset(wps_raw[:].bitcast(I32), 0)
+        nc.vector.memset(wb_s[:].bitcast(I32), 0)
         nc.vector.memset(w2_s_raw[1][:].bitcast(I32), 0)
         make_identity(nc, ident[:])
-        make_identity(nc, ident_bf[:])
+        nc.gpsimd.dma_start(out=b_sb[:], in_=b.rearrange("(p t) -> p t", t=4))
+
+        half = C * Z // 2
+        width = 2 * CQ * Z
+
+        def load_small_scales(tile, scales, q):
+            nc.sync.dma_start(
+                out=tile[32 * q : 32 * q + 4, :].rearrange("p (g n) -> p g n", g=2).bitcast(I32),
+                in_=scales[:, 4 * q : 4 * q + 4, :].rearrange("g q n -> q g n").bitcast(I32),
+            )
+
+        def load_w2_scales(h, q):
+            nc.sync.dma_start(
+                out=w2_s_raw[h][32 * q : 32 * q + 4, :].bitcast(I32),
+                in_=w2_scales[0, 4 * q : 4 * q + 4, h * half : (h + 1) * half].bitcast(I32),
+            )
+
+        def load_w2_words(q):
+            nc.sync.dma_start(out=w2_raw[q][:].bitcast(I32), in_=w2_words[0, :, q * width : (q + 1) * width].bitcast(I32))
 
         nc.sync.dma_start(out=phib0[:], in_=phi_bytes[0:P, :])
-        nc.sync.dma_start(out=pscale[:], in_=phi_scale.rearrange("i j -> (i j)").partition_broadcast(P))
-        nc.sync.dma_start(
-            out=wp_raw[:].rearrange("p (g n) -> p g n", g=2).bitcast(I32),
-            in_=wp_words.rearrange("g p n -> p g n").bitcast(I32),
-        )
+        nc.sync.dma_start(out=pscale_row[0:1, :], in_=phi_scale.rearrange("i j -> (i j)").unsqueeze(0))
+        nc.sync.dma_start(out=wp_raw[:].rearrange("p (g n) -> p g n", g=2).bitcast(I32), in_=wp_words.rearrange("g p n -> p g n").bitcast(I32))
         nc.sync.dma_start(out=z_bf[:], in_=z.rearrange("(r p) k -> p r k", p=P))
         nc.sync.dma_start(out=wz_sb[:], in_=wz)
-        nc.sync.dma_start(out=b_sb[:], in_=b.rearrange("(p t) -> p t", t=4))
         for q in range(4):
-            nc.gpsimd.dma_start(
-                out=wps_raw[32 * q : 32 * q + 4, :].rearrange("p (g n) -> p g n", g=2).bitcast(I32),
-                in_=wp_scales[:, 4 * q : 4 * q + 4, :].rearrange("g q n -> q g n").bitcast(I32),
-            )
+            load_w2_scales(0, q)
+        for q in range(4):
+            load_small_scales(wps_raw, wp_scales, q)
+        load_w2_words(0)
+        load_w2_words(1)
+        nc.sync.dma_start(out=phib_rest[:], in_=phi_bytes[P:, :].rearrange("(r p) k -> p r k", p=P))
+        nc.sync.dma_start(out=wb_w[:].bitcast(I32), in_=wb_words.rearrange("g p n -> p g n").bitcast(I32))
+        for q in range(4):
+            load_w2_scales(1, q)
+        load_w2_words(2)
+        load_w2_words(3)
+        for q in range(4):
+            load_small_scales(wb_s, wb_scales, q)
         nc.gpsimd.tensor_scalar(zs[:], z_bf[:], 1.0 / math.sqrt(Z), 0.0, op0=MULT, op1=ADD)
-        for q in range(4):
-            nc.gpsimd.dma_start(
-                out=wb_s[32 * q : 32 * q + 4, :, :].bitcast(I32),
-                in_=wb_scales[:, 4 * q : 4 * q + 4, :].rearrange("g q n -> q g n").bitcast(I32),
-            )
-        half = C * Z // 2
-        for h in range(2):
-            for q in range(4):
-                nc.sync.dma_start(
-                    out=w2_s_raw[h][32 * q : 32 * q + 4, :].bitcast(I32),
-                    in_=w2_scales[0, 4 * q : 4 * q + 4, h * half : (h + 1) * half].bitcast(I32),
-                )
-            for q in (2 * h, 2 * h + 1):
-                width = 2 * CQ * Z
-                nc.sync.dma_start(
-                    out=w2_raw[q][:].bitcast(I32), in_=w2_words[0, :, q * width : (q + 1) * width].bitcast(I32)
-                )
-            if h == 0:
-                nc.sync.dma_start(out=phib_rest[:], in_=phi_bytes[P:, :].rearrange("(r p) k -> p r k", p=P))
-                nc.sync.dma_start(out=wb_w[:].bitcast(I32), in_=wb_words.rearrange("g p n -> p g n").bitcast(I32))
 
         w2_s_i = w2_s[:].rearrange("p k n -> p (k n)").bitcast(I32).rearrange("p (k c) -> p k c", k=KC)
         w2_w_i = w2_w[:].rearrange("p k n -> p (k n)").bitcast(I32).rearrange("p (k c w) -> p k c w", k=KC, w=2)
 
         def permute_scales(h):
             nc.vector.tensor_copy(
-                out=w2_s_i[:, :, h * C // 2 : (h + 1) * C // 2],
-                in_=w2_s_raw[h][:].bitcast(I32).rearrange("p (c k) -> p k c", k=KC),
+                out=w2_s_i[:, :, h * C // 2 : (h + 1) * C // 2].rearrange("p (o k) c -> p o c k", k=2),
+                in_=w2_s_raw[h][:].bitcast(I32).rearrange("p (c o k) -> p o c k", c=C // 2, k=2),
             )
 
         def permute_words(q):
@@ -204,6 +216,10 @@ def tile_epinetindexedattributerewards_d2p_kernel(
         def quantize_q(r):
             nc.vector.quantize_mx(out=qc[r][:].bitcast(FP8X4), scales=qs[r][:], in_=qg[r][:].rearrange("p n t -> p (n t)"))
 
+        nc.vector.tensor_copy(out=ident_bf[:], in_=ident[:])
+        sbank = ring.tile([P, 32], F32, name="bank")
+        nc.tensor.matmul(sbank[:], lhsT=ones[:], rhs=pscale_row[:], start=True, stop=True)
+        nc.vector.tensor_copy(out=pscale[:], in_=sbank[:])
         widen(0)
         turn(0)
         for g in range(2):
@@ -233,22 +249,28 @@ def tile_epinetindexedattributerewards_d2p_kernel(
         quantize_q(0)
         permute_words(1)
 
-        def pattern(rest, n_scalar, n_gpsimd, tail):
-            share = ["S" if (i + 1) * n_scalar // rest > i * n_scalar // rest else "V" for i in range(rest)]
-            early = [i for i in range(rest - tail) if share[i] == "S"]
+        def pattern(count, n_wide, n_scalar, n_gpsimd, tail):
+            want = {"S": n_scalar, "V": count - n_wide - n_scalar, "W": n_wide}
+            done = {"S": 0, "V": 0, "W": 0}
+            share = []
+            for i in range(count):
+                who = max(want, key=lambda e: want[e] * (i + 1) / count - done[e])
+                done[who] += 1
+                share.append([who, None if who == "V" else "P"])
+            early = [i for i in range(count - tail) if share[i][0] != "V"]
             for n, i in enumerate(early):
                 if (n + 1) * n_gpsimd // len(early) > n * n_gpsimd // len(early):
-                    share[i] = "G"
+                    share[i][1] = "G"
             return share
 
         jobs = []
         for a, sh in ((0, SH_A), (1, SH_B)):
-            jobs += [(a, 0, 2 * i, who, a) for i, who in enumerate(pattern(KC // 2, *sh, 0))]
+            jobs += [(a, 0, 2 * i, who, route, a) for i, (who, route) in enumerate(pattern(KC // 2, *sh, 0))]
         for r in range(1, ROWS):
             sh = SH_L if r == ROWS - 1 else (*SH_F, 0)
-            jobs.insert(len(jobs) - AHEAD, (r + 1, r, 0, "A", None))
-            jobs.insert(len(jobs) - AHEAD + 2, (r + 1, r, 1, "A", None))
-            jobs += [(r + 1, r, i + 2, who, None) for i, who in enumerate(pattern(KC - 2, *sh))]
+            for n in range(NSET):
+                jobs.insert(len(jobs) - AHEAD + n, (r + 1, r, n, "S", "A", None))
+            jobs += [(r + 1, r, i + NSET, who, route, None) for i, (who, route) in enumerate(pattern(KC - NSET, *sh))]
         last_job = {job[0]: pos for pos, job in enumerate(jobs)}
 
         events = {}
@@ -270,14 +292,14 @@ def tile_epinetindexedattributerewards_d2p_kernel(
                 st["first"] = False
 
         def quads(t):
-            return [t[:, n * C : (n + 1) * C] for n in range(KI)]
+            return [t[:, n * C : (n + 1) * C] for n in range(t.shape[1] // C)]
 
         def finish(pos, a, r, half):
             acc_s = small.tile([P, P], F32, name="acc_s")
             st = sums[a]
 
             def step0():
-                turn_sum(a, [p for e in range(min(GACC, st["g"] // 2)) for p in quads(acc_g[a][e])] + quads(acc_v[a][st["v"] % 2]) + quads(acc_v[a][1 - st["v"] % 2]), True)
+                turn_sum(a, [p for e in range(min(GACC, st["g"] // (2 * GW))) for p in quads(acc_g[a][e])] + [p for e in range(min(NSET, st["v"])) for p in quads(acc_v[a][(st["v"] + e) % NSET])], True)
 
             def step1():
                 nc.scalar.copy(acc_s[:], st["tile"][:])
@@ -312,7 +334,7 @@ def tile_epinetindexedattributerewards_d2p_kernel(
                     lhsT=phic[r][:, g * P : (g + 1) * P].bitcast(FP8X4),
                     lhsT_scale=phis[r][:, g * P : (g + 1) * P],
                     rhs=wb_w[:, g, :].bitcast(FP4X4),
-                    rhs_scale=wb_s[:, g, :],
+                    rhs_scale=wb_s[:, g * C : (g + 1) * C],
                     start=(g == 0),
                     stop=(g == 1),
                 )
@@ -330,7 +352,7 @@ def tile_epinetindexedattributerewards_d2p_kernel(
                 pos += step
                 at(pos, lambda r=r, f=f: f(r))
 
-        for pos, (a, r, chunk, who, half) in enumerate(jobs):
+        for pos, (a, r, chunk, who, route, half) in enumerate(jobs):
             for f in events.pop(pos, []):
                 f()
             st = sums[a]
@@ -356,37 +378,65 @@ def tile_epinetindexedattributerewards_d2p_kernel(
             width = 512 // len(parts)
             if who == "V":
                 order = list(enumerate(parts))
-                if st["v"] // 2 % 2:
+                if st["v"] // NSET % 2 and NSET == 2:
                     order.reverse()
                 for n, (k, col) in order:
-                    dst = acc_v[a][st["v"] % 2][:, n * width : (n + 1) * width]
+                    dst = acc_v[a][st["v"] % NSET][:, n * width : (n + 1) * width]
                     zk = zs[:, r, k : k + 1]
-                    if st["v"] < 2 and not st["init"]:
+                    if st["v"] < NSET and not st["init"]:
                         nc.vector.tensor_scalar(dst, col, zk, None, op0=MULT)
                         continue
-                    prior = dst if st["v"] >= 2 else st["init"][st["v"]][:, n * width : (n + 1) * width]
+                    prior = dst if st["v"] >= NSET else st["init"][st["v"]][:, n * width : (n + 1) * width]
                     nc.vector.scalar_tensor_tensor(out=dst, in0=col, scalar=zk, in1=prior, op0=MULT, op1=ADD)
                 st["v"] += 1
             else:
-                prod = prods.tile([P, C * KI], F32, name="prod")
-                for n, (k, col) in enumerate(parts):
-                    nc.scalar.activation(prod[:, n * width : (n + 1) * width], col, ACT.Copy, scale=zs[:, r, k : k + 1])
-                if who == "A":
+                wide = route == "G" and GW == 2
+                if wide and st["g"] % 2:
+                    prod = st["pair"][:, C * KI :]
+                elif wide:
+                    pair = pairs.tile([P, 2 * C * KI], F32, name="pair")
+                    st["pair"] = pair
+                    prod = pair[:, : C * KI]
+                else:
+                    single = prods.tile([P, C * KI], F32, name="prod")
+                    prod = single[:]
+                if who == "S":
+                    for n, (k, col) in enumerate(parts):
+                        nc.scalar.activation(prod[:, n * width : (n + 1) * width], col, ACT.Copy, scale=zs[:, r, k : k + 1])
+                elif half is None:
+                    factor = zs[:, r, KI * chunk : KI * chunk + KI].unsqueeze(2).to_broadcast([P, KI, C])
+                    nc.vector.tensor_tensor(out=prod.rearrange("p (k c) -> p k c", k=KI), in0=cols, in1=factor, op=MULT)
+                else:
+                    factor = zs[:, r, KI * chunk : KI * chunk + 2 * KI].rearrange("p (e k) -> p e k", e=2)
+                    nc.vector.tensor_tensor(
+                        out=prod.rearrange("p (e k c) -> p e k c", e=2, k=KI),
+                        in0=cols,
+                        in1=factor.unsqueeze(3).to_broadcast([P, 2, KI, C // 2]),
+                        op=MULT,
+                    )
+                if route == "A":
                     st["init"].append(prod)
-                elif who == "G":
+                elif wide:
+                    st["g"] += 1
+                    if st["g"] == 2:
+                        st["held"] = [st["pair"]]
+                    elif st["g"] % 2 == 0:
+                        first = st["held"].pop() if st["held"] else acc_g[a][0]
+                        nc.gpsimd.tensor_tensor(out=acc_g[a][0][:], in0=first[:], in1=st["pair"][:], op=ADD)
+                elif route == "G":
                     e = st["g"] // 2 if st["g"] < 2 * GACC else st["g"] % GACC
                     if st["g"] < 2 * GACC and st["g"] % 2 == 0:
                         st["held"] = [prod]
                     else:
                         first = st["held"].pop() if st["g"] < 2 * GACC else acc_g[a][e]
-                        nc.gpsimd.tensor_tensor(out=acc_g[a][e][:], in0=first[:], in1=prod[:], op=ADD)
+                        nc.gpsimd.tensor_tensor(out=acc_g[a][e][:], in0=first[:, :], in1=prod, op=ADD)
                     st["g"] += 1
                 else:
                     st["run"].append(prod)
             done = pos == last_job[a]
             if len(st["run"]) == RUN or (done and st["run"]):
                 pieces = [p for t in st["run"] for p in quads(t)]
-                free_at = last_job[a - 1] + LAG + FIN[1] if a else 0
+                free_at = last_job[a - 1] + LAG + FIN[1] + GAP if a and TACC == 1 else 0
                 at(max(pos + LAG, free_at), lambda pieces=pieces, a=a: turn_sum(a, pieces, False))
                 st["run"] = []
             if done:

import math
from contextlib import ExitStack

import concourse.mybir as mybir
from concourse.masks import make_identity

N, D, H, Z, C = 512, 1024, 512, 128, 128
FLOPS = 2 * N * D * H + 2 * N * Z * H + 2 * N * H * C * Z + 2 * N * C * Z + 2 * N * D * C

F32 = mybir.dt.float32
BF16 = mybir.dt.bfloat16
I32 = mybir.dt.int32
U32 = mybir.dt.uint32
U8 = mybir.dt.uint8
FP8 = mybir.dt.float8_e4m3fn
FP8X4 = mybir.dt.float8_e4m3fn_x4
FP4X4 = mybir.dt.float4_e2m1fn_x4
ADD = mybir.AluOpType.add
MULT = mybir.AluOpType.mult
MAX = mybir.AluOpType.max
ACT = mybir.ActivationFunctionType

P = 128
ROWS = N // P
KI = 4
KC = Z // KI
QUARTERS = 4
CQ = C // QUARTERS

SH_A = (7, 8, 7)
SH_B = (5, 6, 5)
SH_F = (0, 13, 8)
GACC = 1
RUN = 3
LAG = 6
FIN = (11, 11, 13, 16)
SH_L = (0, 13, 6, 7)
RELU_ON = "SSSS"
NSET = 1
GAP = 6
GW = 1
TACC = 1
AHEAD = 7
WID_POS = (0, 34, 68)
PERM_POS = (4, 9, 14)
STEPS = (0, 7, 2, 5, 1, 2, 2, 5)
BASE_POS = 12
WIDEN_ON = "VVSS"


def tile_epinetindexedattributerewards_d2p_kernel(
    tc, phi_bytes, phi_scale, z, wp_words, wp_scales, wz, b, w2_words, w2_scales, wb_words, wb_scales, out
):
    nc = tc.nc
    with ExitStack() as ctx:
        keep = ctx.enter_context(tc.tile_pool(name="keep", bufs=1))
        prods = ctx.enter_context(tc.tile_pool(name="prods", bufs=16))
        pairs = ctx.enter_context(tc.tile_pool(name="pairs", bufs=6))
        small = ctx.enter_context(tc.tile_pool(name="small", bufs=2))
        ring = ctx.enter_context(tc.psum_pool(name="ring", bufs=8 - TACC))
        tacc = ctx.enter_context(tc.psum_pool(name="tacc", bufs=TACC))
        ctx.enter_context(tc.manual_schedule())

        ident = keep.tile([P, P], F32, name="ident", align_bytes=64)
        ident_bf = keep.tile([P, P], BF16, name="ident_bf", align_bytes=64)
        pscale = keep.tile([P, 32], F32, name="pscale")
        z_bf = keep.tile([P, ROWS, Z], BF16, name="z_bf")
        zs = keep.tile([P, ROWS, Z], F32, name="zs")
        z_t = keep.tile([P, N], BF16, name="z_t")
        wp_raw = keep.tile([P, 2 * 2 * H], U8, name="wp_raw", align_bytes=64)
        wp_w = keep.tile([P, 2, 4, 256], U8, name="wp_w", align_bytes=64)
        wps_raw = keep.tile([P, 2 * H], U8, name="wps_raw", align_bytes=64)
        wp_s = keep.tile([P, 2, 4, P], U8, name="wp_s", align_bytes=64)
        wz_sb = keep.tile([P, H], BF16, name="wz_sb", align_bytes=64)
        b_sb = keep.tile([P, 4], BF16, name="b_sb")
        ones = keep.tile([P, P], F32, name="ones", align_bytes=64)
        pscale_row = keep.tile([P, 32], F32, name="pscale_row", align_bytes=64)
        wb_w = keep.tile([P, 2, 256], U8, name="wb_w", align_bytes=64)
        wb_s = keep.tile([P, 2 * C], U8, name="wb_s", align_bytes=64)
        w2_s_raw = [keep.tile([P, C * Z // 2], U8, name=f"w2_s_raw{h}", align_bytes=64) for h in range(2)]
        w2_s = keep.tile([P, KC, C * KI], U8, name="w2_s", align_bytes=64)
        w2_w = keep.tile([P, KC, 2 * C * KI], U8, name="w2_w", align_bytes=64)
        w2_raw = [keep.tile([P, 2 * CQ * Z], U8, name=f"w2_raw{q}", align_bytes=64) for q in range(QUARTERS)]
        phib0 = keep.tile([P, D], U8, name="phib0", align_bytes=64)
        phib_rest = keep.tile([P, ROWS - 1, D], U8, name="phib_rest", align_bytes=64)
        phib = [phib0[:]] + [phib_rest[:, r, :] for r in range(ROWS - 1)]
        phi_bf = [keep.tile([P, D], BF16, name=f"phi_bf{r}", align_bytes=64) for r in range(ROWS)]
        phig = [keep.tile([P, 2, P, 4], BF16, name=f"phig{r}", align_bytes=64) for r in range(ROWS)]
        phic = [keep.tile([P, 2 * P], U32, name=f"phic{r}", align_bytes=64) for r in range(ROWS)]
        phis = [keep.tile([P, 2 * P], U8, name=f"phis{r}", align_bytes=64) for r in range(ROWS)]
        zwb = keep.tile([P, 4, N], F32, name="zwb")
        hsum = [keep.tile([P, 4, P], F32, name=f"hsum{r}") for r in range(ROWS)]
        qg = [keep.tile([P, P, 4], BF16, name=f"qg{r}", align_bytes=64) for r in range(ROWS)]
        qc = [keep.tile([P, P], U32, name=f"qc{r}", align_bytes=64) for r in range(ROWS)]
        qs = [keep.tile([P, P], U8, name=f"qs{r}", align_bytes=64) for r in range(ROWS)]
        base = keep.tile([P, ROWS, C], F32, name="base")
        acc_v = [[keep.tile([P, KI * C], F32, name=f"acc_v{a}_{e}") for e in range(2)] for a in range(ROWS + 1)]
        acc_g = [[keep.tile([P, GW * KI * C], F32, name=f"acc_g{a}_{e}") for e in range(GACC)] for a in range(ROWS + 1)]

        nc.vector.memset(pscale_row[:], 0.0)
        nc.gpsimd.memset(ones[:], 1.0)
        nc.vector.memset(w2_s_raw[0][:].bitcast(I32), 0)
        nc.vector.memset(wps_raw[:].bitcast(I32), 0)
        nc.vector.memset(wb_s[:].bitcast(I32), 0)
        nc.vector.memset(w2_s_raw[1][:].bitcast(I32), 0)
        make_identity(nc, ident[:])
        nc.gpsimd.dma_start(out=b_sb[:], in_=b.rearrange("(p t) -> p t", t=4))

        half = C * Z // 2
        width = 2 * CQ * Z

        def load_small_scales(tile, scales, q):
            nc.sync.dma_start(
                out=tile[32 * q : 32 * q + 4, :].rearrange("p (g n) -> p g n", g=2).bitcast(I32),
                in_=scales[:, 4 * q : 4 * q + 4, :].rearrange("g q n -> q g n").bitcast(I32),
            )

        def load_w2_scales(h, q):
            nc.sync.dma_start(
                out=w2_s_raw[h][32 * q : 32 * q + 4, :].bitcast(I32),
                in_=w2_scales[0, 4 * q : 4 * q + 4, h * half : (h + 1) * half].bitcast(I32),
            )

        def load_w2_words(q):
            nc.sync.dma_start(out=w2_raw[q][:].bitcast(I32), in_=w2_words[0, :, q * width : (q + 1) * width].bitcast(I32))

        nc.sync.dma_start(out=phib0[:], in_=phi_bytes[0:P, :])
        nc.sync.dma_start(out=pscale_row[0:1, :], in_=phi_scale.rearrange("i j -> (i j)").unsqueeze(0))
        nc.sync.dma_start(out=wp_raw[:].rearrange("p (g n) -> p g n", g=2).bitcast(I32), in_=wp_words.rearrange("g p n -> p g n").bitcast(I32))
        nc.sync.dma_start(out=z_bf[:], in_=z.rearrange("(r p) k -> p r k", p=P))
        nc.sync.dma_start(out=wz_sb[:], in_=wz)
        for q in range(4):
            load_w2_scales(0, q)
        for q in range(4):
            load_small_scales(wps_raw, wp_scales, q)
        load_w2_words(0)
        load_w2_words(1)
        nc.sync.dma_start(out=phib_rest[:], in_=phi_bytes[P:, :].rearrange("(r p) k -> p r k", p=P))
        nc.sync.dma_start(out=wb_w[:].bitcast(I32), in_=wb_words.rearrange("g p n -> p g n").bitcast(I32))
        for q in range(4):
            load_w2_scales(1, q)
        load_w2_words(2)
        load_w2_words(3)
        for q in range(4):
            load_small_scales(wb_s, wb_scales, q)
        nc.gpsimd.tensor_scalar(zs[:], z_bf[:], 1.0 / math.sqrt(Z), 0.0, op0=MULT, op1=ADD)

        w2_s_i = w2_s[:].rearrange("p k n -> p (k n)").bitcast(I32).rearrange("p (k c) -> p k c", k=KC)
        w2_w_i = w2_w[:].rearrange("p k n -> p (k n)").bitcast(I32).rearrange("p (k c w) -> p k c w", k=KC, w=2)

        def permute_scales(h):
            nc.vector.tensor_copy(
                out=w2_s_i[:, :, h * C // 2 : (h + 1) * C // 2].rearrange("p (o k) c -> p o c k", k=2),
                in_=w2_s_raw[h][:].bitcast(I32).rearrange("p (c o k) -> p o c k", c=C // 2, k=2),
            )

        def permute_words(q):
            nc.vector.tensor_copy(
                out=w2_w_i[:, :, q * CQ : (q + 1) * CQ, :],
                in_=w2_raw[q][:].bitcast(I32).rearrange("p (c k w) -> p k c w", k=KC, w=2),
            )

        def widen(r):
            for j in range(D // P):
                cols = slice(j * P, (j + 1) * P)
                src = phib[r][:, cols].bitcast(FP8)
                factor = pscale[:, 8 * r + j : 8 * r + j + 1]
                if WIDEN_ON[r] == "V":
                    nc.vector.tensor_scalar(phi_bf[r][:, cols], src, factor, None, op0=MULT)
                else:
                    nc.scalar.activation(phi_bf[r][:, cols], src, ACT.Copy, scale=factor)

        def turn(r):
            bank = ring.tile([P, 2, 2, P], F32, name="bank")
            words = phi_bf[r][:].bitcast(F32)
            for g in range(2):
                for u in range(2):
                    nc.tensor.transpose(bank[:, g, u, :], words[:, 256 * g + u : 256 * (g + 1) : 2], ident[:])
            for g in range(2):
                nc.scalar.copy(
                    phig[r][:, g, :, :].rearrange("p n j -> p (n j)").bitcast(F32).rearrange("p (n u) -> p n u", u=2),
                    bank[:, g, :, :].rearrange("p u n -> p n u"),
                )

        def quantize_phi(r):
            nc.vector.quantize_mx(
                out=phic[r][:].bitcast(FP8X4), scales=phis[r][:], in_=phig[r][:].rearrange("p g n j -> p (g n j)")
            )

        hbanks = {}

        def hidden_mm(r):
            bank = ring.tile([P, 4, P], F32, name="bank")
            hbanks[r] = bank
            for t in range(4):
                for g in range(2):
                    nc.tensor.matmul_mx(
                        out=bank[:, t, :],
                        lhsT=wp_w[:, g, t, :].bitcast(FP4X4),
                        lhsT_scale=wp_s[:, g, t, :],
                        rhs=phic[r][:, g * P : (g + 1) * P].bitcast(FP8X4),
                        rhs_scale=phis[r][:, g * P : (g + 1) * P],
                        start=(g == 0),
                        stop=(g == 1),
                    )

        def hidden_add(r):
            nc.vector.tensor_tensor(out=hsum[r][:], in0=hbanks[r][:], in1=zwb[:, :, r * P : (r + 1) * P], op=ADD)

        def hidden_relu(r):
            if RELU_ON[r] == "S":
                nc.scalar.activation(qg[r][:], hsum[r][:].rearrange("p t n -> p n t"), ACT.Relu)
            else:
                nc.gpsimd.tensor_scalar(qg[r][:], hsum[r][:].rearrange("p t n -> p n t"), 0.0, 0.0, op0=MAX, op1=ADD)

        def quantize_q(r):
            nc.vector.quantize_mx(out=qc[r][:].bitcast(FP8X4), scales=qs[r][:], in_=qg[r][:].rearrange("p n t -> p (n t)"))

        nc.vector.tensor_copy(out=ident_bf[:], in_=ident[:])
        sbank = ring.tile([P, 32], F32, name="bank")
        nc.tensor.matmul(sbank[:], lhsT=ones[:], rhs=pscale_row[:], start=True, stop=True)
        nc.vector.tensor_copy(out=pscale[:], in_=sbank[:])
        widen(0)
        turn(0)
        for g in range(2):
            nc.vector.tensor_copy(
                out=wp_w[:, g, :, :].rearrange("p t (m b) -> p t m b", b=2),
                in_=wp_raw[:, g * 1024 : (g + 1) * 1024].rearrange("p (m t b) -> p t m b", t=4, b=2),
            )
        quantize_phi(0)
        for g in range(2):
            nc.vector.tensor_copy(
                out=wp_s[:, g, :, :], in_=wps_raw[:, g * H : (g + 1) * H].rearrange("p (m t) -> p t m", t=4)
            )
        zbank = ring.tile([P, N], BF16, name="bank")
        for r in range(ROWS):
            nc.tensor.transpose(zbank[:, r * P : (r + 1) * P], z_bf[:, r, :], ident_bf[:])
        nc.scalar.copy(z_t[:], zbank[:])
        wz_t = wz_sb[:].rearrange("z (m t) -> z t m", t=4)
        for t in range(4):
            bank = ring.tile([P, N], F32, name="bank")
            nc.tensor.matmul(bank[:], lhsT=wz_t[:, t, :], rhs=z_t[:], start=True, stop=True)
            nc.scalar.activation(zwb[:, t, :], bank[:], ACT.Identity, bias=b_sb[:, t : t + 1])
        hidden_mm(0)
        permute_scales(0)
        hidden_add(0)
        hidden_relu(0)
        permute_words(0)
        quantize_q(0)
        permute_words(1)

        def pattern(count, n_wide, n_scalar, n_gpsimd, tail):
            want = {"S": n_scalar, "V": count - n_wide - n_scalar, "W": n_wide}
            done = {"S": 0, "V": 0, "W": 0}
            share = []
            for i in range(count):
                who = max(want, key=lambda e: want[e] * (i + 1) / count - done[e])
                done[who] += 1
                share.append([who, None if who == "V" else "P"])
            early = [i for i in range(count - tail) if share[i][0] != "V"]
            for n, i in enumerate(early):
                if (n + 1) * n_gpsimd // len(early) > n * n_gpsimd // len(early):
                    share[i][1] = "G"
            return share

        jobs = []
        for a, sh in ((0, SH_A), (1, SH_B)):
            jobs += [(a, 0, 2 * i, who, route, a) for i, (who, route) in enumerate(pattern(KC // 2, *sh, 0))]
        for r in range(1, ROWS):
            sh = SH_L if r == ROWS - 1 else (*SH_F, 0)
            for n in range(NSET):
                jobs.insert(len(jobs) - AHEAD + n, (r + 1, r, n, "S", "A", None))
            jobs += [(r + 1, r, i + NSET, who, route, None) for i, (who, route) in enumerate(pattern(KC - NSET, *sh))]
        last_job = {job[0]: pos for pos, job in enumerate(jobs)}

        events = {}

        def at(pos, f):
            events.setdefault(pos, []).append(f)

        sums = [{"first": True, "tile": None, "v": 0, "g": 0, "held": [], "run": [], "init": []} for a in range(ROWS + 1)]

        def turn_sum(a, pieces, last):
            st = sums[a]
            if st["tile"] is None:
                acc_t = tacc.tile([P, P], F32, name="acc_t")
                st["tile"] = acc_t
            for n, piece in enumerate(pieces):
                nc.tensor.matmul(
                    st["tile"][:], lhsT=piece, rhs=ident[:], is_transpose=True, start=st["first"], stop=(last and n == len(pieces) - 1)
                )
                st["first"] = False

        def quads(t):
            return [t[:, n * C : (n + 1) * C] for n in range(t.shape[1] // C)]

        def finish(pos, a, r, half):
            acc_s = small.tile([P, P], F32, name="acc_s")
            st = sums[a]

            def step0():
                turn_sum(a, [p for e in range(min(GACC, st["g"] // (2 * GW))) for p in quads(acc_g[a][e])] + [p for e in range(min(NSET, st["v"])) for p in quads(acc_v[a][(st["v"] + e) % NSET])], True)

            def step1():
                nc.scalar.copy(acc_s[:], st["tile"][:])

            def step2():
                back = ring.tile([P, P], F32, name="bank")
                st["back"] = back
                nc.tensor.transpose(back[:], acc_s[:], ident[:])

            def step3():
                back = st["back"]
                if half is None:
                    res = small.tile([P, C], F32, name="res")
                    nc.vector.tensor_tensor(out=res[:], in0=back[:], in1=base[:, r, :], op=ADD)
                    nc.sync.dma_start(out=out[r * P : (r + 1) * P, :], in_=res[:])
                else:
                    cols = slice(half * C // 2, (half + 1) * C // 2)
                    part = small.tile([P, C // 2], F32, name="part")
                    hres = small.tile([P, C // 2], F32, name="hres")
                    nc.vector.tensor_tensor(out=part[:], in0=back[:, 0 : C // 2], in1=base[:, r, cols], op=ADD)
                    nc.vector.tensor_tensor(out=hres[:], in0=back[:, C // 2 : C], in1=part[:], op=ADD)
                    nc.sync.dma_start(out=out[r * P : (r + 1) * P, cols], in_=hres[:])

            for lag, f in zip(FIN, (step0, step1, step2, step3)):
                at(pos + lag, f)

        def base_rows(r):
            bbank = ring.tile([P, C], F32, name="bank")
            for g in range(2):
                nc.tensor.matmul_mx(
                    out=bbank[:],
                    lhsT=phic[r][:, g * P : (g + 1) * P].bitcast(FP8X4),
                    lhsT_scale=phis[r][:, g * P : (g + 1) * P],
                    rhs=wb_w[:, g, :].bitcast(FP4X4),
                    rhs_scale=wb_s[:, g * C : (g + 1) * C],
                    start=(g == 0),
                    stop=(g == 1),
                )
            nc.scalar.copy(base[:, r, :], bbank[:])


        at(PERM_POS[0], lambda: permute_scales(1))
        at(PERM_POS[1], lambda: permute_words(2))
        at(PERM_POS[2], lambda: permute_words(3))
        at(BASE_POS, lambda: base_rows(0))
        for r in range(1, ROWS):
            chain = (widen, turn, quantize_phi, hidden_mm, hidden_add, hidden_relu, quantize_q, base_rows)
            pos = WID_POS[r - 1]
            for step, f in zip(STEPS, chain):
                pos += step
                at(pos, lambda r=r, f=f: f(r))

        for pos, (a, r, chunk, who, route, half) in enumerate(jobs):
            for f in events.pop(pos, []):
                f()
            st = sums[a]
            bank = ring.tile([P, C * KI], F32, name="bank")
            if half is None:
                spans = [(chunk, slice(0, 512), slice(0, 512))]
                cols = bank[:].rearrange("p (c k) -> p k c", k=KI)
                parts = [(KI * chunk + k, cols[:, k, :]) for k in range(KI)]
            else:
                spans = [(chunk + e, slice(256 * e, 256 * e + 256), slice(256 * half, 256 * half + 256)) for e in range(2)]
                cols = bank[:].rearrange("p (e c k) -> p e k c", e=2, k=KI)
                parts = [(KI * (chunk + e) + k, cols[:, e, k, :]) for e in range(2) for k in range(KI)]
            for kc, dst, src in spans:
                nc.tensor.matmul_mx(
                    out=bank[:, dst],
                    lhsT=qc[r][:].bitcast(FP8X4),
                    lhsT_scale=qs[r][:],
                    rhs=w2_w[:, kc, 2 * src.start : 2 * src.stop].bitcast(FP4X4),
                    rhs_scale=w2_s[:, kc, src],
                    start=True,
                    stop=True,
                )
            width = 512 // len(parts)
            if who == "V":
                order = list(enumerate(parts))
                if st["v"] // NSET % 2 and NSET == 2:
                    order.reverse()
                for n, (k, col) in order:
                    dst = acc_v[a][st["v"] % NSET][:, n * width : (n + 1) * width]
                    zk = zs[:, r, k : k + 1]
                    if st["v"] < NSET and not st["init"]:
                        nc.vector.tensor_scalar(dst, col, zk, None, op0=MULT)
                        continue
                    prior = dst if st["v"] >= NSET else st["init"][st["v"]][:, n * width : (n + 1) * width]
                    nc.vector.scalar_tensor_tensor(out=dst, in0=col, scalar=zk, in1=prior, op0=MULT, op1=ADD)
                st["v"] += 1
            else:
                wide = route == "G" and GW == 2
                if wide and st["g"] % 2:
                    prod = st["pair"][:, C * KI :]
                elif wide:
                    pair = pairs.tile([P, 2 * C * KI], F32, name="pair")
                    st["pair"] = pair
                    prod = pair[:, : C * KI]
                else:
                    single = prods.tile([P, C * KI], F32, name="prod")
                    prod = single[:]
                if who == "S":
                    for n, (k, col) in enumerate(parts):
                        nc.scalar.activation(prod[:, n * width : (n + 1) * width], col, ACT.Copy, scale=zs[:, r, k : k + 1])
                elif half is None:
                    factor = zs[:, r, KI * chunk : KI * chunk + KI].unsqueeze(2).to_broadcast([P, KI, C])
                    nc.vector.tensor_tensor(out=prod.rearrange("p (k c) -> p k c", k=KI), in0=cols, in1=factor, op=MULT)
                else:
                    factor = zs[:, r, KI * chunk : KI * chunk + 2 * KI].rearrange("p (e k) -> p e k", e=2)
                    nc.vector.tensor_tensor(
                        out=prod.rearrange("p (e k c) -> p e k c", e=2, k=KI),
                        in0=cols,
                        in1=factor.unsqueeze(3).to_broadcast([P, 2, KI, C // 2]),
                        op=MULT,
                    )
                if route == "A":
                    st["init"].append(prod)
                elif wide:
                    st["g"] += 1
                    if st["g"] == 2:
                        st["held"] = [st["pair"]]
                    elif st["g"] % 2 == 0:
                        first = st["held"].pop() if st["held"] else acc_g[a][0]
                        nc.gpsimd.tensor_tensor(out=acc_g[a][0][:], in0=first[:], in1=st["pair"][:], op=ADD)
                elif route == "G":
                    e = st["g"] // 2 if st["g"] < 2 * GACC else st["g"] % GACC
                    if st["g"] < 2 * GACC and st["g"] % 2 == 0:
                        st["held"] = [prod]
                    else:
                        first = st["held"].pop() if st["g"] < 2 * GACC else acc_g[a][e]
                        nc.gpsimd.tensor_tensor(out=acc_g[a][e][:], in0=first[:, :], in1=prod, op=ADD)
                    st["g"] += 1
                else:
                    st["run"].append(prod)
            done = pos == last_job[a]
            if len(st["run"]) == RUN or (done and st["run"]):
                pieces = [p for t in st["run"] for p in quads(t)]
                free_at = last_job[a - 1] + LAG + FIN[1] + GAP if a and TACC == 1 else 0
                at(max(pos + LAG, free_at), lambda pieces=pieces, a=a: turn_sum(a, pieces, False))
                st["run"] = []
            if done:
                if st["held"]:
                    at(pos + LAG, lambda pieces=quads(st["held"][0]), a=a: turn_sum(a, pieces, False))
                finish(pos + LAG, a, r, half)
        for pos in sorted(events):
            for f in events[pos]:
                f()
